import numpy as np, ml_dtypes
CORES = [5,29,101,125,133,157,229,253]
N = 8
import mx_ref
BF = ml_dtypes.bfloat16
def pick(q, e):
    c = np.concatenate([q[0].reshape(128, -1, 4), np.zeros((128, 1, 4), np.uint8)], axis=1); s = np.concatenate([q[1], np.ones((16, 1), np.uint8)], axis=1)
    return (np.ascontiguousarray(c[:, e].reshape(128, -1)), np.ascontiguousarray(s[:, e]))
def join(*qs):
    return (np.concatenate([q[0] for q in qs], axis=1), np.concatenate([q[1] for q in qs], axis=1))
def put(q, e, v):
    c, s = q[0].reshape(128, -1, 4).copy(), q[1].copy(); c[:, e] = v[0].reshape(128, -1, 4); s[:, e] = v[1]
    return (c.reshape(128, -1), s)
def pk(c, s):
    return (np.ascontiguousarray(c), mx_ref.live(s))
def emit(q):
    return q[0], q[1]
def packed(v, rng):
    q = [mx_ref.quantize(np.ascontiguousarray(v[r])) for r in range(N)]
    return np.stack([a for a, b in q]), np.stack([mx_ref.plane(b, rng) for a, b in q])
def tile(rs):
    return np.stack(rs, axis=2).reshape(128, -1).astype(BF)
def f(rng, *shape):
    return mx_ref.flush((rng.standard_normal(shape, dtype=np.float32) * np.exp2(rng.integers(-2, 3, shape[:-1] + (1,)))).astype(BF))
def wide(rng, *shape, cols=0):
    v = rng.standard_normal(shape, dtype=np.float32) * np.exp2(rng.integers(-12, 13, shape)).astype(np.float32)
    if cols: v *= np.repeat(np.exp2(rng.integers(-cols, cols + 1, shape[:-2] + (1, shape[-1] // 4))) * (rng.random(shape[:-2] + (1, shape[-1] // 4)) > 0.0625), 4, axis=-1).astype(np.float32)
    return mx_ref.flush(v.astype(BF))
P, CAPP, LAST = 128, 48, 4
def times(t, v):
    return mx_ref.flush((t.astype(np.float32) * np.asarray(v, np.float32)).astype(BF))
def weights(rng, v):
    c, p = packed(times(f(rng, N, 128, 4096), v), rng)
    return {"wc": c, "ws": p}
def plain(rng):
    return {"x": f(rng, N, 128, 4 * P), "u": np.stack([f(rng, 128, 512)] * N), **weights(rng, 0.25)}
def tagged(rng, al, be, lo):
    d = plain(rng)
    x, u = np.array(d["x"]), np.array(d["u"])
    x[:, :24] = 0
    for p, v in ((0, al), (8, be), (16, lo)): x[:, p, ::4] = np.asarray(v, np.float32).astype(BF)
    u[:, :, :8] = 0
    u[:, 0, 0] = 2.0 ** 21
    u[:, 8, 4] = 2.0 ** 21
    u[:, 16, 4] = 1.0
    keep = ~np.isin(np.arange(1024) % 128, (0, 8, 16))
    return {"x": x, "u": u, **weights(rng, 0.25 * np.repeat(keep, 4))}
def setup_inputs(rng):
    return plain(rng)
def setup_inputs_ties(rng):
    return tagged(rng, rng.integers(-1, 1, (N, P)), rng.integers(-1, 1, (N, P)), np.zeros((N, P)))
def setup_inputs_near(rng):
    place = np.zeros((N, P), int) + np.arange(P)
    early = place < CAPP
    al = np.where(early, -((place + int(rng.integers(0, 2))) % 2), 4 * rng.integers(0, 2, (N, P)))
    lo = rng.integers(0, 8, (N, P))
    lo[0] = np.minimum(lo[0], 6)
    lo[1] = 7
    return tagged(rng, al, np.where(early, 0, 4), np.where(early, 0, lo))
def setup_inputs_crowd(rng):
    b = np.concatenate([[N - 1], rng.permutation(N - 2) + 1, [N]])
    a = np.where(np.roll(b, -1) > np.roll(b, -2), 16, -16)
    one = np.ones((1, P), int)
    a, b = a[:, None] * one, b[:, None] * one
    a[N - 3] = 16
    a[N - 2, P - 1] = -16
    a[N - 1, :CAPP - 1] = -16
    a[N - 1, P - 1] = -16
    b[N - 1, P - 1] = -16
    return tagged(rng, a, b, 0 * b)
def setup_inputs_huge(rng):
    d = plain(rng)
    sign = np.repeat(np.where(rng.random((N, 1, P)) < 0.25, -1.0, 1.0), 4, axis=2)
    u = np.array(d["u"])
    u[:, :, :8] = (-(1 + rng.random((128, 8))) * 2.0 ** 29).astype(np.float32).astype(BF)
    x = ((1 + rng.random((N, 128, 4 * P))) * 2.0 ** 27 * sign).astype(np.float32).astype(BF)
    return {"x": x, "u": u, **weights(rng, 0.125)}
def setup_inputs_spread(rng):
    return {**plain(rng), "x": wide(rng, N, 128, 4 * P, cols=6)}
def check_inputs(d):
    b = []
    for k in ("x", "u"):
        v = np.abs(d[k].astype(np.float32))
        if not (np.isfinite(v).all() and ((v == 0) | (v >= 2.0 ** -30) & (v <= 2.0 ** 30)).all()): b.append("a value of " + k)
    v = d["u"].astype(np.float32)
    if (v != v[:1]).any(): b.append("u isn't the same on every rank")
    return b
def reference(x, u, wc, ws):
    y, sp = np.zeros((N, 128, (LAST - 1) * P), np.float32), np.zeros((N, 1, (LAST - 1) * P), np.float32)
    oc, osc = np.zeros((N, 128, 4 * P), np.uint8), np.zeros((N, 16, P), np.uint8)
    tu = [mx_ref.quantize(np.ascontiguousarray(u[r])) for r in range(N)]
    wt = [[pick(pk(wc[r], ws[r]), np.arange(128 * m, 128 * m + 128)) for m in range(8)] for r in range(N)]
    cell = {1: [mx_ref.quantize(np.ascontiguousarray(x[r])) for r in range(N)]}
    got = {1: [mx_ref.matmul(tu[r], cell[1][r]) for r in range(N)]}
    for w in range(2, LAST + 1):
        cell[w], got[w] = [], []
        for r in range(N):
            home = [(r + k) % N for k in range(w)]
            at = [(np.arange(P) + (r + k) // N) % P for k in range(w)]
            score = np.stack([got[k][r][0] + got[w - k][home[k]][1][at[k]] for k in range(1, w)]) + np.float32(0)
            best = 1 + np.argmax(score, axis=0)
            slots, left, right = [], [], []
            for k in range(1, w):
                e = np.flatnonzero(best == k)[:CAPP]
                sp[r, 0, (w - 2) * P + e] = k
                fill = np.full(CAPP - len(e), -1)
                slots.append(np.concatenate([e, fill]))
                left.append(pick(cell[k][r], slots[-1]))
                right.append(pick(cell[w - k][home[k]], np.concatenate([at[k][e], fill])))
            a, b = join(*left), join(*right)
            z = [np.maximum(mx_ref.matmul(wt[r][t], a) + mx_ref.matmul(wt[r][4 + t], b), np.float32(0)) * np.float32(0.05) for t in range(4)]
            new = mx_ref.quantize(np.ascontiguousarray(tile(z)))
            e = np.concatenate(slots)
            used = np.flatnonzero(e >= 0)
            cell[w].append(put(cell[w - 1][r], e[used], pick(new, used)))
            got[w].append(mx_ref.matmul(tu[r], cell[w][r]))
            y[r, :, (w - 2) * P:(w - 1) * P] = got[w][r]
    for r in range(N): oc[r], osc[r] = emit(cell[LAST][r])
    return {"y": y, "oc": oc, "osc": osc, "sp": sp}

@@ -1,0 +1,410 @@
+import numpy as np
+from concourse.mybir import dt, AluOpType, ActivationFunctionType
+
+A, F = AluOpType, ActivationFunctionType
+P, CAPP = 128, 48
+X4, U8, BF, F32, I32, U16 = "float8_e4m3fn_x4", "uint8", "bfloat16", "float32", "int32", "uint16"
+K1, K2, C2, C1, C1R, OWN = 0, 128, 256, 384, 528, 656
+L2, N1, N2, S3, SRV = 0, 48, 176, 304, 432
+
+
+def _pair(name, n):
+    return {name + "q": ("sbuf", [128, n], X4), name + "s": ("sbuf", [128, n], U8)}
+
+
+SCRATCH = {"ps": ("psum", [128, 4096], F32)}
+for _n, _w in (("wt", 1024), ("u0", 128), ("uab", 256), ("own", OWN), ("srv", SRV), ("lw", 512), ("out", 128),
+               ("right", 128), ("left", 128), ("c4", 128), ("h1", 128), ("h2", CAPP), ("h4", 128)):
+    SCRATCH.update(_pair(_n, _w))
+for _n, _w, _d in (("xt", 528, BF), ("xt2", 512, BF), ("ut", 512, BF), ("t2", 512, BF), ("t3", 512, BF), ("t5", 512, BF),
+                   ("i1", 128, I32), ("i1b", 128, I32), ("i2", 8, I32), ("i3", 1, I32), ("i3b", 1, I32),
+                   ("maskf", 128, F32), ("maskb", 128, BF), ("thr", 128, BF), ("hold", 128, F32), ("d0", 128, BF),
+                   ("col", 4, F32), ("tab", 64, F32), ("kt", 384, BF), ("k3t", 384, BF), ("tt", 256, BF),
+                   ("c48", 128, BF), ("c96", 128, BF), ("offu", 16, U16), ("off3", 8, U16), ("off4", 16, U16), ("off5", 8, U16),
+                   ("s2", 128, F32), ("fl", 128, BF), ("nf", 128, BF), ("cap", 256, BF), ("hh", 144, BF), ("dd", 128, BF),
+                   ("vv", 128, BF), ("sc", 128, BF), ("exa", 384, F32), ("exb", 384, F32), ("eya", 384, F32), ("eyb", 384, F32),
+                   ("m1s", 16, F32), ("m3s", 8, F32), ("m1h", 16, F32), ("m3h", 8, F32), ("m1", 16, F32), ("m3", 8, F32),
+                   ("lsh", 8, U16), ("ls", 8, U16), ("sm", 128, F32), ("kk", 128, BF), ("ee", 384, BF), ("cum", 384, BF),
+                   ("zz", 128, BF), ("sc5", 128, BF), ("tk", 128, BF), ("spb", 384, F32), ("yb", 384, F32)):
+    SCRATCH[_n] = ("sbuf", [128, _w], _d)
+
+HOPS = ["a1", "a2", "a3", "a4", "b1", "b2", "b4", "c1", "c4"]
+SEMAPHORES = (["cv", "cs", "loc", "n1", "n2", "l2", "m1", "m3", "r4", "ls"] + ["h" + h for h in HOPS]
+              + ["e%d" % i for i in range(110)])
+
+
+def _mask(engines):
+    m = 0
+    for e in engines:
+        m |= 1 << e
+    return m
+
+
+def _helpers(T, topo, r):
+    n = len(T.cores)
+    me, prev, nxt = T.cores[r], T.cores[(r - 1) % n], T.cores[(r + 1) % n]
+    ok = [c for c in topo.cores_of(me) if c != me and topo.may_write(c, prev) and topo.may_write(c, nxt)]
+    ok.sort(key=lambda c: topo.die(c) != topo.die(me))
+    return ok[:3]
+
+
+def _send(g, T, topo, src, dst, out, in_, sem, engines):
+    rid, pid = topo.addr(dst, src)
+    g.remote_dma(out, in_, T.sem[sem], T.sem.loc, pid, rid, _mask(engines))
+    return len(engines)
+
+
+def _b(v):
+    return v.bitcast(dt.uint8)
+
+
+def _relay(g, core, T, topo, r, role):
+    n = len(T.cores)
+    prev, nxt = T.cores[(r - 1) % n], T.cores[(r + 1) % n]
+    on = len(topo.engines(T.cores[r], core))
+    jobs = {0: [("ha1", on // 2, prev, _b(T.srvq[:, N1:N1 + P]), _b(T.h1q[:]), "n1"),
+                ("ha2", on // 2, prev, _b(T.srvq[:, L2:L2 + CAPP]), _b(T.h2q[:]), "l2"),
+                ("ha3", on, nxt, T.m3[:], T.m3h[:], "m3"),
+                ("ha4", on // 2, prev, _b(T.rightq[:]), _b(T.h4q[:]), "r4")],
+            1: [("hb1", on // 2, prev, T.srvs[:, N1:N1 + P], T.h1s[:], "n1"),
+                ("hb2", on // 2, prev, T.srvs[:, L2:L2 + CAPP], T.h2s[:], "l2"),
+                ("hb4", on // 2, prev, T.rights[:], T.h4s[:], "r4")],
+            2: [("hc1", on // 2, nxt, T.m1[:], T.m1h[:], "m1"),
+                ("hc4", on // 2, prev, T.ls[:], T.lsh[:], "ls")]}[role]
+    sent = 0
+    for sem, cnt, dst, out, in_, rsem in jobs:
+        g.wait_ge(T.sem[sem], cnt)
+        sent += _send(g, T, topo, core, dst, out, in_, rsem, topo.engines(core, dst))
+    g.wait_ge(T.sem.loc, sent)
+
+
+def rank_program(g, core, T, topo):
+    n = len(T.cores)
+    r = T.rank_of(core)
+    if r is None:
+        for k in range(n):
+            h = _helpers(T, topo, k)
+            if core in h:
+                _relay(g, core, T, topo, k, h.index(core))
+        return
+    prev2 = T.cores[(r - 2) % n]
+    ra, rb, rc = _helpers(T, topo, r)
+    on = topo.engines(core, ra)
+    lo, hi = on[:len(on) // 2], on[len(on) // 2:]
+    far_a = len(topo.engines(_helpers(T, topo, (r + 1) % n)[0], core))
+    far2 = len(topo.engines(T.cores[(r + 2) % n], core))
+    last = r == n - 1
+    d1 = 1 if r == 0 else 0
+    d2 = 1 if r < 2 else 0
+    scale = float(np.float32(0.05))
+
+    q = {"v": g.vector, "s": g.scalar, "t": g.tensor, "y": g.sync, "g": g}
+    cnt, waited, pool = {}, {}, [0]
+
+    def wait(e, toks):
+        for s, c in toks:
+            if s in ("cv", "cs"):
+                c = cnt[s]
+            if waited.get((e, s), 0) < c:
+                q[e].wait_ge(T.sem[s], c)
+                waited[(e, s)] = c
+
+    def fresh():
+        pool[0] += 1
+        return "e%d" % (pool[0] - 1)
+
+    def op(e, fn, deps=(), sig=None, inc=1):
+        wait(e, deps)
+        s = "c" + e if sig is None else (fresh() if sig is True else sig)
+        fn().then_inc(T.sem[s], inc)
+        cnt[s] = cnt.get(s, 0) + inc
+        return (s, cnt[s])
+
+    v, s_, pe = g.vector, g.scalar, g.tensor
+
+    def dma(e, out, in_, deps=(), sig=True):
+        return op(e, lambda: q[e].dma_start(out, in_), deps, sig, 16)
+
+    def quant(name, c, nn, in_, deps, sig=None):
+        return op("v", lambda: v.quantize_mx(T[name + "q"][:, c:c + nn], T[name + "s"][:, c:c + nn], in_), deps, sig)
+
+    def pickq(dst, c, src, a, b, off, nn, deps, sig=True):
+        return op("v", lambda: v.tensor_copy(T[dst + "q"][:, c:c + nn].bitcast(dt.uint32),
+                                             T[src + "q"][:, a:b].bitcast(dt.uint32).indirect(off)), deps, sig)
+
+    def picks(dst, c, src, a, b, off, nn, deps, sig=True):
+        return op("s", lambda: s_.activation(T[dst + "s"][:, c:c + nn], T[src + "s"][:, a:b].indirect(off), F.Copy), deps, sig)
+
+    def bank(b, a=0, e=P):
+        return T.ps[:, 512 * b + a:512 * b + e]
+
+    def mm(b, st, sc, mv, mc, nn, start, stop, deps=()):
+        def fn():
+            return pe.matmul_mx(bank(b, 0, nn), T[st + "q"][:, sc:sc + P], T[st + "s"][:, sc:sc + P],
+                                T[mv + "q"][:, mc:mc + nn], T[mv + "s"][:, mc:mc + nn], start, stop)
+        if stop:
+            return op("t", fn, deps, True)
+        wait("t", deps)
+        fn()
+        return None
+
+    def ts(out, in0, s1, o0, s2=None, o1=None, deps=(), sig=None):
+        if o1 is None:
+            return op("v", lambda: v.tensor_scalar(out, in0, s1, None, o0), deps, sig)
+        return op("v", lambda: v.tensor_scalar(out, in0, s1, s2, o0, o1), deps, sig)
+
+    def tt(out, a, b, o, deps=(), sig=None):
+        return op("v", lambda: v.tensor_tensor(out, a, b, o), deps, sig)
+
+    def cp(out, in_, deps=(), sig=None):
+        return op("v", lambda: v.tensor_copy(out, in_), deps, sig)
+
+    def ms(out, c, deps=(), sig=None):
+        return op("v", lambda: v.memset(out, c), deps, sig)
+
+    def scan(out, a, b, init, o0, o1, deps=(), sig=None):
+        return op("v", lambda: v.tensor_tensor_scan(out, a, b, init, o0, o1), deps, sig)
+
+    def relu(e, tile, t, c0, c1, p0, deps, sig):
+        out, in_ = tile[:, 4 * c0 + t:4 * c1:4], bank(t, p0, p0 + c1 - c0)
+        if e == "v":
+            return ts(out, in_, 0.0, A.max, scale, A.mult, deps, sig)
+        return op("s", lambda: s_.activation(out, in_, F.Relu, scale=scale), deps, sig)
+
+    sent = [0]
+
+    def send(dst, out, in_, sem, engines, deps):
+        wait("g", deps)
+        sent[0] += _send(g, T, topo, core, dst, out, in_, sem, engines)
+
+    CV = ("cv", 0)
+    lx = [dma("y", T.xt[:, 8:520], T.x[:])]
+    if d2:
+        lx.append(dma("s", T.xt[:, 520:528], T.x[:, 0:8]))
+    lr = dma("s", T.xt[:, 4:8], T.x[:, 508:512]) if last else None
+    lu = dma("s", T.ut[:], T.u[:])
+    lw = [dma("y", _b(T.wtq[:]), T.wc[:]), dma("s", T.wts[:], T.ws[:])]
+    lb = dma("s", T.xt2[:, 4 * CAPP:], T.x[:, 4 * CAPP:])
+    io = fresh()
+    op("g", lambda: g.iota(T.i1[:], [[1, P]], P, -1), (), io)
+    op("g", lambda: g.iota(T.i2[:], [[16, 8]], 0, 0), (), io)
+    io = op("g", lambda: g.iota(T.i3[:], [[1, 1]], 0, 1), (), io)
+    ou = fresh()
+    ms(T.offu[:, 0:8], 0, sig=ou)
+    ou = ms(T.offu[:, 8:16], 1, sig=ou)
+    for k in range(3):
+        ms(T.kt[:, P * k:P * k + P], float(k + 1))
+        ms(T.k3t[:, P * k:P * k + P], float((k + 1) % 3))
+    ms(T.tt[:, 0:P], 0.0)
+    ms(T.tt[:, P:], 1.0)
+    ms(T.c48[:], float(CAPP))
+    ms(T.c96[:], float(2 * CAPP))
+    ms(T.hh[:, 0:16], 0.0)
+    ms(T.hold[:], 1.0)
+    ms(T.d0[:], -100.0)
+    ms(T.spb[:, 0:CAPP], 1.0)
+    ms(T.spb[:, CAPP:P], 0.0)
+
+    n1c = P + 2 * d2
+    c1 = quant("own", C1, n1c, T.xt[:, 8:8 + 4 * n1c], lx, True)
+    send(ra, _b(T.h1q[:]), _b(T.ownq[:, C1 + d1:C1 + d1 + P]), "ha1", hi, [c1])
+    send(rb, T.h1s[:], T.owns[:, C1 + d1:C1 + d1 + P], "hb1", lo, [])
+    e2 = topo.engines(core, prev2)
+    send(prev2, _b(T.srvq[:, N2:N2 + P]), _b(T.ownq[:, C1 + d2:C1 + d2 + P]), "n2", e2, [])
+    send(prev2, T.srvs[:, N2:N2 + P], T.owns[:, C1 + d2:C1 + d2 + P], "n2", e2, [])
+    qu = quant("u0", 0, P, T.ut[:], [lu], True)
+    ua = [pickq("uab", 0, "u0", 0, P, T.offu[:], 256, [qu, ou]), picks("uab", 0, "u0", 0, P, T.offu[:], 256, [qu, ou])]
+    l1 = quant("lw", 0, P, T.xt[:, 8:520], [], True)
+    c1r = quant("own", C1R, P, T.xt[:, 4:516], [lr], True) if last else c1
+    lcol = C1R if last else C1
+
+    ts(T.i1b[:], T.i1[:], 15, A.bitwise_and, deps=[io])
+    ts(T.i3b[:], T.i3[:], 15, A.bitwise_and)
+    ts(T.hold[:, 0:P:16], T.i2[:], 0.0, A.mult, deps=[CV])
+    ts(T.d0[:, 0:P:16], T.i2[:], 1.0 / P, A.mult)
+    ts(T.maskf[:], T.i1b[:], 0.0, A.is_equal)
+    ts(T.maskb[:], T.i1b[:], 0.0, A.is_equal)
+    for k in range(3):
+        ts(T.col[:, k:k + 1], T.i3b[:], float(P * k), A.add)
+
+    def tab(k):
+        return T.tab[:, 8 * k:8 * k + 8]
+    t8, qv, pl, o1, o21, tmp, tmp2 = (tab(k) for k in range(7))
+    ts(T.thr[:], T.maskf[:], CAPP + 0.5 - 1000.0, A.mult, 1000.0, A.add, deps=[CV])
+    ts(t8, T.i2[:], T.col[:, 0:1], A.add)
+
+    def turned(out, in_, d):
+        ts(tmp, in_, P - d - 0.5, A.is_gt, -float(P), A.mult, deps=[CV])
+        ts(tmp2, in_, float(d), A.add)
+        tt(out, tmp, tmp2, A.add, deps=[CV])
+    turned(qv, t8, d1)
+    turned(pl, qv, 1 if last else 0)
+    ts(o1, qv, float(S3), A.add, deps=[CV])
+    tt(tmp, pl, qv, A.subtract)
+    ts(tmp2, pl, CAPP - 0.5, A.is_lt)
+    ts(tmp, tmp, float(L2 - N1), A.add, deps=[CV])
+    tt(tmp, tmp, tmp2, A.mult, deps=[CV])
+    ts(o21, tmp, float(N1 - S3), A.add, deps=[CV])
+
+    for t in range(4):
+        mm(t, "wt", P * t, "own", C1, P, True, False, lw + [c1])
+    mm(4, "uab", 0, "own", C1, P, True, False, ua)
+    n1 = ("n1", 2 * far_a)
+    b1 = [mm(t, "wt", 512 + P * t, "srv", N1, P, False, True, [n1]) for t in (0, 2, 1, 3)]
+    b1 = [b1[0], b1[2], b1[1], b1[3]]
+    s1e = mm(4, "uab", P, "srv", N1, P, False, True)
+    ga = fresh()
+    for t in (0, 2, 1, 3):
+        ga_ = relu("v" if t < 2 else "s", T.xt2, t, 0, CAPP, 0, [b1[t], lb], ga)
+    c2 = quant("own", C2, P, T.xt2[:], [ga_], True)
+    send(ra, _b(T.h2q[:]), _b(T.ownq[:, C2:C2 + CAPP]), "ha2", hi, [c2])
+    send(rb, T.h2s[:], T.owns[:, C2:C2 + CAPP], "hb2", lo, [])
+    l2c = quant("lw", P, P, T.xt2[:], [], True)
+    gb = fresh()
+    b0 = CAPP - 1 if last else CAPP
+    for t in (0, 2, 1, 3):
+        gb_ = relu("v" if t < 2 else "s", T.t3, t, b0, P, b0, [ga_], gb)
+
+    n2 = ("n2", 2 * far2)
+    mm(5, "uab", 0, "own", C2, P, True, False, [c2])
+    s2p = mm(5, "uab", P, "srv", N2, P, False, True, [n2])
+    a12 = mm(7, "uab", 0, "lw", 0, 2 * P, True, True, [l1, l2c])
+    b2 = []
+    for t in range(4):
+        mm(t, "wt", P * t, "own", C2, P, True, False, [gb_])
+        b2.append(mm(t, "wt", 512 + P * t, "srv", N2, P, False, True))
+    g2 = fresh()
+    for t in range(4):
+        g2_ = relu("s", T.t2, t, 0, P, 0, [b2[t]], g2)
+    for t in range(4):
+        mm(t, "wt", P * t, "own", lcol, P, True, False, [g2_, c1r])
+    mm(6, "uab", 0, "own", lcol, P, True, False)
+    for k in range(2):
+        tt(T.exa[:, P * k:P * k + P], bank(7, P * k, P * k + P), T.maskf[:], A.mult, deps=[a12, CV] if k == 0 else [])
+    s2c = cp(T.s2[:], bank(5), [s2p], True)
+    wait("v", [CV])
+    for k in range(2):
+        scan(T.exb[:, P * k:P * k + P], T.hold[:], T.exa[:, P * k:P * k + P], 0.0, A.mult, A.add)
+    fe = tt(T.fl[:], T.s2[:], bank(4), A.is_gt, [s1e, s2c], True)
+    m1s = cp(T.m1s[:], T.exb[:, 15:2 * P:16], [CV], True)
+    send(rc, T.m1h[:], T.m1s[:], "hc1", lo, [m1s])
+    k2 = quant("own", K2, P, T.t2[:], [g2_], True)
+
+    l2 = ("l2", 2 * far_a)
+    s1l = mm(6, "uab", P, "srv", L2, P, False, True, [l2])
+    b3 = [mm(t, "wt", 512 + P * t, "srv", L2, P, False, True) for t in range(4)]
+    late = [(0, CAPP - 1, 1), (P - 1, P, 0)] if last else [(0, CAPP, 0)]
+    g3 = fresh()
+    for t in range(4):
+        for a, b, p0 in late:
+            g3_ = relu("s", T.t3, t, a, b, p0, [b3[t], gb_], g3)
+    fa = fresh()
+    for a, b, p0 in late:
+        fa_ = tt(T.fl[:, a:b], T.s2[:, a:b], bank(6, p0, p0 + b - a), A.is_gt, [s1l, fe], fa)
+    ts(T.nf[:], T.fl[:], -2.0, A.mult, 2.0, A.add, deps=[fa_])
+    scan(T.cap[:, 0:P], T.fl[:], T.c48[:], 0.0, A.add, A.min)
+    scan(T.cap[:, P:], T.nf[:], T.c96[:], 0.0, A.add, A.min, [CV])
+    tt(T.hh[:, 1:P + 1], T.cap[:, 0:P], T.cap[:, P:], A.add, [CV])
+    tt(T.dd[:], T.hh[:, 1:P + 1], T.hh[:, 0:P], A.subtract, [CV])
+    tt(T.vv[:], T.dd[:], T.maskb[:], A.mult, [CV])
+    k1 = quant("own", K1, P, T.t3[:], [g3_], True)
+    scan(T.sc[:], T.d0[:], T.vv[:], -1.0, A.max, A.subtract, [CV])
+    o3 = ts(T.off3[:], T.sc[:, 15:P:16], float(P), A.mult, T.col[:, 2:3], A.add, [CV], True)
+    dp = [o3, k1, k2, c2]
+    c3 = [pickq("lw", 2 * P, "own", 0, 3 * P, T.off3[:], P, dp), picks("lw", 2 * P, "own", 0, 3 * P, T.off3[:], P, dp)]
+    c3s = [pickq("srv", S3, "own", 0, 3 * P, T.off3[:], P, dp), picks("srv", S3, "own", 0, 3 * P, T.off3[:], P, dp)]
+    a3 = mm(5, "uab", 0, "lw", 2 * P, P, True, True, c3 + [s2c])
+    bs = mm(6, "uab", P, "srv", 0, SRV, True, True, c3s + [fa_])
+    y23 = mm(4, "u0", 0, "lw", P, 2 * P, True, True, [fe])
+    tt(T.exa[:, 2 * P:], bank(5), T.maskf[:], A.mult, [a3])
+    scan(T.exb[:, 2 * P:], T.hold[:], T.exa[:, 2 * P:], 0.0, A.mult, A.add, [CV])
+    m3s = cp(T.m3s[:], T.exb[:, 2 * P + 15:3 * P:16], [CV], True)
+    send(ra, T.m3h[:], T.m3s[:], "ha3", on, [m3s])
+    yc = op("s", lambda: s_.activation(T.yb[:, 0:2 * P], bank(4, 0, 2 * P), F.Copy), [y23], True)
+    dma("y", T.y[:, 0:2 * P], T.yb[:, 0:2 * P], [yc])
+
+    def src_col(k, p):
+        qq = (p + d1) % P
+        if k == 0:
+            return S3 + qq
+        if k == 2:
+            return N2 + qq
+        pp = (qq + (1 if last else 0)) % P
+        return L2 + pp if pp < CAPP else N1 + qq
+    wait("v", [bs])
+    for k in range(3):
+        a = 0
+        for p in range(1, P + 1):
+            if p == P or src_col(k, p) != src_col(k, p - 1) + 1:
+                c = src_col(k, a)
+                tt(T.eya[:, P * k + a:P * k + p], bank(6, c, c + p - a), T.maskf[:, a:p], A.mult)
+                a = p
+    wait("v", [CV])
+    for k in range(3):
+        scan(T.eyb[:, P * k:P * k + P], T.hold[:], T.eya[:, P * k:P * k + P], 0.0, A.mult, A.add)
+    sp3 = cp(T.spb[:, P:2 * P], T.k3t[:].indirect(T.off3[:]), [], True)
+    dma("y", T.sp[0:1, 0:2 * P], T.spb[0:1, 0:2 * P], [sp3])
+
+    def sm(k, w=1):
+        return T.sm[:, 8 * k:8 * (k + w)]
+    tt(sm(0, 2), T.m1[:], T.eyb[:, 15:2 * P:16], A.add, [("m1", far_a), CV])
+    cp(sm(2), T.eyb[:, 2 * P + 15:3 * P:16])
+    tt(sm(3), sm(1), sm(0), A.is_gt, [CV])
+    tt(sm(4), sm(1), sm(0), A.max)
+    tt(sm(5), sm(3), o21, A.mult, [CV])
+    ts(sm(6), sm(3), float(P), A.mult)
+    tt(sm(7), sm(5), o1, A.add, [CV])
+    tt(sm(8), sm(6), t8, A.add)
+    ts(sm(9), sm(5), -1.0, A.mult, float(N2 - S3), A.add)
+    ts(sm(10), sm(6), -1.0, A.mult, float(2 * P), A.add)
+    wait("v", [CV])
+    tt(sm(11), T.m3[:], sm(2), A.add, [("m3", far_a)])
+    tt(sm(12), sm(11), sm(4), A.is_gt, [CV])
+    tt(sm(13), sm(12), sm(9), A.mult, [CV])
+    tt(sm(14), sm(12), sm(10), A.mult)
+    tt(sm(0, 2), sm(13, 2), sm(7, 2), A.add, [CV])
+    o4 = cp(T.off4[:], sm(0, 2), [CV], True)
+    dp = [o4, n1, n2, l2] + c3s
+    oq = pickq("out", 0, "srv", 0, SRV, T.off4[:, 0:8], P, dp)
+    osc = picks("out", 0, "srv", 0, SRV, T.off4[:, 0:8], P, dp)
+    send(rc, T.lsh[:], T.off4[:, 8:16], "hc4", lo, [o4])
+    send(ra, _b(T.h4q[:]), _b(T.outq[:]), "ha4", hi, [oq])
+    send(rb, T.h4s[:], T.outs[:], "hb4", lo, [osc])
+
+    ls = ("ls", far_a)
+    dp = [ls, l1, l2c] + c3
+    lf = [pickq("left", 0, "lw", 0, 3 * P, T.ls[:], P, dp), picks("left", 0, "lw", 0, 3 * P, T.ls[:], P, dp)]
+    for t in range(4):
+        mm(t, "wt", 512 + P * t, "right", 0, P, True, False, [g3_, ("r4", 2 * far_a)])
+    b5 = [mm(t, "wt", P * t, "left", 0, P, False, True, lf) for t in range(4)]
+    g5 = fresh()
+    for t in range(4):
+        g5_ = relu("s", T.t5, t, 0, P, 0, [b5[t]], g5)
+    cp(T.kk[:], T.kt[:].indirect(T.ls[:]))
+    wait("v", [CV])
+    for k in range(3):
+        ts(T.ee[:, P * k:P * k + P], T.kk[:], float(k + 1), A.is_equal)
+    wait("v", [CV])
+    for k in range(3):
+        scan(T.cum[:, P * k:P * k + P], T.ee[:, P * k:P * k + P], T.c96[:], 0.0, A.add, A.min)
+    tt(T.zz[:], T.cum[:].indirect(T.ls[:]), T.thr[:], A.is_gt, [CV])
+    scan(T.sc5[:], T.d0[:], T.zz[:], -1.0, A.max, A.subtract, [CV])
+    o5 = ts(T.off5[:], T.sc5[:, 15:P:16], float(P), A.mult, T.col[:, 1:2], A.add, [CV], True)
+    cp(T.tk[:], T.tt[:].indirect(T.off5[:]), [o5])
+    sp4 = tt(T.spb[:, 2 * P:], T.tk[:], T.kk[:], A.mult, [CV], True)
+    dma("y", T.sp[0:1, 2 * P:], T.spb[0:1, 2 * P:], [sp4])
+    q5 = quant("lw", 3 * P, P, T.t5[:], [g5_], True)
+    dp = [o5, q5]
+    c4q = pickq("c4", 0, "lw", 2 * P, 4 * P, T.off5[:], P, dp)
+    c4s = picks("c4", 0, "lw", 2 * P, 4 * P, T.off5[:], P, dp)
+    y4 = mm(7, "u0", 0, "c4", 0, P, True, True, [c4q, c4s, m1s])
+    dma("y", T.oc[:], _b(T.c4q[:]), [c4q])
+    for k in range(4):
+        dma("s", T.osc[4 * k:4 * k + 4, :], T.c4s[32 * k:32 * k + 4, :], [c4s])
+    y4c = cp(T.yb[:, 2 * P:], bank(7), [y4], True)
+    dma("y", T.y[:, 2 * P:], T.yb[:, 2 * P:], [y4c])
+
+    g.wait_ge(T.sem.loc, sent[0])
+    for s, c in cnt.items():
+        if max([w for (e, s2), w in waited.items() if s2 == s] + [0]) < c:
+            wait(s[1] if s in ("cv", "cs") else "g", [(s, c)])

@@ -4,8 +4,10 @@ from concourse.mybir import dt, AluOpType, ActivationFunctionType
 A, F = AluOpType, ActivationFunctionType
 P, CAPP = 128, 48
 X4, U8, BF, F32, I32, U16 = "float8_e4m3fn_x4", "uint8", "bfloat16", "float32", "int32", "uint16"
-K1, K2, C2, C1, C1R, OWN = 0, 128, 256, 384, 528, 656
-L2, N1, N2, S3, SRV = 0, 48, 176, 304, 432
+K2, C2, K1, C1, C1R, OWN = 0, 128, 256, 384, 528, 656
+N1, N2, L2, S3, SRV = 0, 48, 176, 304, 432
+REST = P - CAPP
+LIFT = 64
 
 
 def _pair(name, n):
@@ -14,22 +16,23 @@ def _pair(name, n):
 
 SCRATCH = {"ps": ("psum", [128, 4096], F32)}
 for _n, _w in (("wt", 1024), ("u0", 128), ("uab", 256), ("own", OWN), ("srv", SRV), ("lw", 512), ("out", 128),
-               ("right", 128), ("left", 128), ("c4", 128), ("h1", 128), ("h2", CAPP), ("h4", 128)):
+               ("right", 128), ("left", 128), ("c4", 128), ("h0", REST), ("h1", CAPP), ("h2", CAPP), ("h4", 128)):
     SCRATCH.update(_pair(_n, _w))
 for _n, _w, _d in (("xt", 528, BF), ("xt2", 512, BF), ("ut", 512, BF), ("t2", 512, BF), ("t3", 512, BF), ("t5", 512, BF),
-                   ("i1", 128, I32), ("i1b", 128, I32), ("i2", 8, I32), ("i3", 1, I32), ("i3b", 1, I32),
+                   ("i1", 128, I32), ("i1b", 128, I32), ("i2", 8, I32), ("i3", 1, I32), ("i3b", 1, I32), ("i4", 128, I32),
                    ("maskf", 128, F32), ("maskb", 128, BF), ("thr", 128, BF), ("hold", 128, F32), ("d0", 128, BF),
-                   ("col", 4, F32), ("tab", 64, F32), ("kt", 384, BF), ("k3t", 384, BF), ("tt", 256, BF),
-                   ("c48", 128, BF), ("c96", 128, BF), ("offu", 16, U16), ("off3", 8, U16), ("off4", 16, U16), ("off5", 8, U16),
-                   ("s2", 128, F32), ("fl", 128, BF), ("nf", 128, BF), ("cap", 256, BF), ("hh", 144, BF), ("dd", 128, BF),
+                   ("col", 4, F32), ("tab", 64, F32), ("kt", 384, BF), ("k3t", 384, BF), ("kz", 256, BF),
+                   ("c48", 128, BF), ("c96", 128, BF), ("gt", 128, BF),
+                   ("offu", 16, U16), ("off3", 8, U16), ("off4", 16, U16), ("off5", 8, U16),
+                   ("s2", 128, F32), ("fl", 128, BF), ("cap", 256, BF), ("hh", 144, BF), ("dd", 128, BF),
                    ("vv", 128, BF), ("sc", 128, BF), ("exa", 384, F32), ("exb", 384, F32), ("eya", 384, F32), ("eyb", 384, F32),
                    ("m1s", 16, F32), ("m3s", 8, F32), ("m1h", 16, F32), ("m3h", 8, F32), ("m1", 16, F32), ("m3", 8, F32),
-                   ("lsh", 8, U16), ("ls", 8, U16), ("sm", 128, F32), ("kk", 128, BF), ("ee", 384, BF), ("cum", 384, BF),
-                   ("zz", 128, BF), ("sc5", 128, BF), ("tk", 128, BF), ("spb", 384, F32), ("yb", 384, F32)):
+                   ("lsh", 8, U16), ("ls", 8, U16), ("sm", 128, F32), ("ee", 384, BF), ("cum", 384, BF),
+                   ("zz", 128, BF), ("sc5", 128, BF), ("spb", 384, F32), ("yb", 384, F32)):
     SCRATCH[_n] = ("sbuf", [128, _w], _d)
 
-HOPS = ["a1", "a2", "a3", "a4", "b1", "b2", "b4", "c1", "c4"]
-SEMAPHORES = (["cv", "cs", "loc", "n1", "n2", "l2", "m1", "m3", "r4", "ls"] + ["h" + h for h in HOPS]
+HOPS = ["a1", "a2", "a3", "a4", "b1", "b2", "b4", "c0", "c1", "c4"]
+SEMAPHORES = (["cv", "cs", "loc", "n1", "n2", "nb", "l2", "m1", "m3", "r4", "ls"] + ["h" + h for h in HOPS]
               + ["e%d" % i for i in range(110)])
 
 
@@ -62,18 +65,21 @@ def _relay(g, core, T, topo, r, role):
     n = len(T.cores)
     prev, nxt = T.cores[(r - 1) % n], T.cores[(r + 1) % n]
     on = len(topo.engines(T.cores[r], core))
-    jobs = {0: [("ha1", on // 2, prev, _b(T.srvq[:, N1:N1 + P]), _b(T.h1q[:]), "n1"),
+    jobs = {0: [("ha1", on // 2, prev, _b(T.srvq[:, N1:N1 + CAPP]), _b(T.h1q[:]), "n1"),
                 ("ha2", on // 2, prev, _b(T.srvq[:, L2:L2 + CAPP]), _b(T.h2q[:]), "l2"),
                 ("ha3", on, nxt, T.m3[:], T.m3h[:], "m3"),
                 ("ha4", on // 2, prev, _b(T.rightq[:]), _b(T.h4q[:]), "r4")],
-            1: [("hb1", on // 2, prev, T.srvs[:, N1:N1 + P], T.h1s[:], "n1"),
+            1: [("hb1", on // 2, prev, T.srvs[:, N1:N1 + CAPP], T.h1s[:], "n1"),
                 ("hb2", on // 2, prev, T.srvs[:, L2:L2 + CAPP], T.h2s[:], "l2"),
                 ("hb4", on // 2, prev, T.rights[:], T.h4s[:], "r4")],
-            2: [("hc1", on // 2, nxt, T.m1[:], T.m1h[:], "m1"),
+            2: [("hc0", on, prev, _b(T.srvq[:, L2 + CAPP:L2 + P]), _b(T.h0q[:]), "nb"),
+                ("hc0", 0, prev, T.srvs[:, L2 + CAPP:L2 + P], T.h0s[:], "nb"),
+                ("hc1", on // 2, nxt, T.m1[:], T.m1h[:], "m1"),
                 ("hc4", on // 2, prev, T.ls[:], T.lsh[:], "ls")]}[role]
     sent = 0
     for sem, cnt, dst, out, in_, rsem in jobs:
-        g.wait_ge(T.sem[sem], cnt)
+        if cnt:
+            g.wait_ge(T.sem[sem], cnt)
         sent += _send(g, T, topo, core, dst, out, in_, rsem, topo.engines(core, dst))
     g.wait_ge(T.sem.loc, sent)
 
@@ -165,8 +171,8 @@ def rank_program(g, core, T, topo):
     def scan(out, a, b, init, o0, o1, deps=(), sig=None):
         return op("v", lambda: v.tensor_tensor_scan(out, a, b, init, o0, o1), deps, sig)
 
-    def relu(e, tile, t, c0, c1, p0, deps, sig):
-        out, in_ = tile[:, 4 * c0 + t:4 * c1:4], bank(t, p0, p0 + c1 - c0)
+    def relu(e, tile, t, c0, c1, p0, deps, sig, b0=0):
+        out, in_ = tile[:, 4 * c0 + t:4 * c1:4], bank(b0 + t, p0, p0 + c1 - c0)
         if e == "v":
             return ts(out, in_, 0.0, A.max, scale, A.mult, deps, sig)
         return op("s", lambda: s_.activation(out, in_, F.Relu, scale=scale), deps, sig)
@@ -182,11 +188,13 @@ def rank_program(g, core, T, topo):
     if d2:
         lx.append(dma("s", T.xt[:, 520:528], T.x[:, 0:8]))
     lr = dma("s", T.xt[:, 4:8], T.x[:, 508:512]) if last else None
+    lwa = dma("y", _b(T.wtq[:, 0:512]), T.wc[:, 0:2048])
+    lws = dma("s", T.wts[:], T.ws[:])
+    lwb = dma("y", _b(T.wtq[:, 512:]), T.wc[:, 2048:])
     lu = dma("s", T.ut[:], T.u[:])
-    lw = [dma("y", _b(T.wtq[:]), T.wc[:]), dma("s", T.wts[:], T.ws[:])]
-    lb = dma("s", T.xt2[:, 4 * CAPP:], T.x[:, 4 * CAPP:])
     io = fresh()
     op("g", lambda: g.iota(T.i1[:], [[1, P]], P, -1), (), io)
+    op("g", lambda: g.iota(T.i4[:], [[1, P]], LIFT + 1 - CAPP, 0), (), io)
     op("g", lambda: g.iota(T.i2[:], [[16, 8]], 0, 0), (), io)
     io = op("g", lambda: g.iota(T.i3[:], [[1, 1]], 0, 1), (), io)
     ou = fresh()
@@ -194,12 +202,11 @@ def rank_program(g, core, T, topo):
     ou = ms(T.offu[:, 8:16], 1, sig=ou)
     for k in range(3):
         ms(T.kt[:, P * k:P * k + P], float(k + 1))
-        ms(T.k3t[:, P * k:P * k + P], float((k + 1) % 3))
-    ms(T.tt[:, 0:P], 0.0)
-    ms(T.tt[:, P:], 1.0)
+        ms(T.k3t[:, P * k:P * k + P], float((k + 2) % 3))
+    ms(T.kz[:, 0:P], 0.0)
     ms(T.c48[:], float(CAPP))
     ms(T.c96[:], float(2 * CAPP))
-    ms(T.hh[:, 0:16], 0.0)
+    ms(T.hh[:, 0:16], float(LIFT))
     ms(T.hold[:], 1.0)
     ms(T.d0[:], -100.0)
     ms(T.spb[:, 0:CAPP], 1.0)
@@ -207,19 +214,21 @@ def rank_program(g, core, T, topo):
 
     n1c = P + 2 * d2
     c1 = quant("own", C1, n1c, T.xt[:, 8:8 + 4 * n1c], lx, True)
-    send(ra, _b(T.h1q[:]), _b(T.ownq[:, C1 + d1:C1 + d1 + P]), "ha1", hi, [c1])
-    send(rb, T.h1s[:], T.owns[:, C1 + d1:C1 + d1 + P], "hb1", lo, [])
+    send(ra, _b(T.h1q[:]), _b(T.ownq[:, C1 + d1:C1 + d1 + CAPP]), "ha1", hi, [c1])
+    send(rb, T.h1s[:], T.owns[:, C1 + d1:C1 + d1 + CAPP], "hb1", lo, [])
     e2 = topo.engines(core, prev2)
     send(prev2, _b(T.srvq[:, N2:N2 + P]), _b(T.ownq[:, C1 + d2:C1 + d2 + P]), "n2", e2, [])
     send(prev2, T.srvs[:, N2:N2 + P], T.owns[:, C1 + d2:C1 + d2 + P], "n2", e2, [])
-    qu = quant("u0", 0, P, T.ut[:], [lu], True)
-    ua = [pickq("uab", 0, "u0", 0, P, T.offu[:], 256, [qu, ou]), picks("uab", 0, "u0", 0, P, T.offu[:], 256, [qu, ou])]
+    send(rc, _b(T.h0q[:]), _b(T.ownq[:, C1 + CAPP:C1 + P]), "hc0", hi, [])
+    send(rc, T.h0s[:], T.owns[:, C1 + CAPP:C1 + P], "hc0", lo, [])
+    lb = cp(T.xt2[:, 4 * CAPP:], T.xt[:, 8 + 4 * CAPP:520], [], True)
     l1 = quant("lw", 0, P, T.xt[:, 8:520], [], True)
     c1r = quant("own", C1R, P, T.xt[:, 4:516], [lr], True) if last else c1
     lcol = C1R if last else C1
 
     ts(T.i1b[:], T.i1[:], 15, A.bitwise_and, deps=[io])
     ts(T.i3b[:], T.i3[:], 15, A.bitwise_and)
+    cp(T.gt[:], T.i4[:])
     ts(T.hold[:, 0:P:16], T.i2[:], 0.0, A.mult, deps=[CV])
     ts(T.d0[:, 0:P:16], T.i2[:], 1.0 / P, A.mult)
     ts(T.maskf[:], T.i1b[:], 0.0, A.is_equal)
@@ -241,81 +250,71 @@ def rank_program(g, core, T, topo):
     turned(pl, qv, 1 if last else 0)
     ts(o1, qv, float(S3), A.add, deps=[CV])
     tt(tmp, pl, qv, A.subtract)
-    ts(tmp2, pl, CAPP - 0.5, A.is_lt)
-    ts(tmp, tmp, float(L2 - N1), A.add, deps=[CV])
-    tt(tmp, tmp, tmp2, A.mult, deps=[CV])
-    ts(o21, tmp, float(N1 - S3), A.add, deps=[CV])
+    ts(o21, tmp, float(L2 - S3), A.add, deps=[CV])
+    qu = quant("u0", 0, P, T.ut[:], [lu], True)
+    ua = [pickq("uab", 0, "u0", 0, P, T.offu[:], 256, [qu, ou]), picks("uab", 0, "u0", 0, P, T.offu[:], 256, [qu, ou])]
 
     for t in range(4):
-        mm(t, "wt", P * t, "own", C1, P, True, False, lw + [c1])
-    mm(4, "uab", 0, "own", C1, P, True, False, ua)
+        mm(t, "wt", P * t, "own", C1, P, True, False, [lwa, lws, c1])
     n1 = ("n1", 2 * far_a)
-    b1 = [mm(t, "wt", 512 + P * t, "srv", N1, P, False, True, [n1]) for t in (0, 2, 1, 3)]
+    n2 = ("n2", 2 * far2)
+    b1 = [mm(t, "wt", 512 + P * t, "srv", N1, P, False, True, [lwb, n1, n2]) for t in (0, 2, 1, 3)]
     b1 = [b1[0], b1[2], b1[1], b1[3]]
-    s1e = mm(4, "uab", P, "srv", N1, P, False, True)
+    for t in range(4):
+        mm(4 + t, "wt", 512 + P * t, "srv", N2, P, True, False)
     ga = fresh()
     for t in (0, 2, 1, 3):
-        ga_ = relu("v" if t < 2 else "s", T.xt2, t, 0, CAPP, 0, [b1[t], lb], ga)
-    c2 = quant("own", C2, P, T.xt2[:], [ga_], True)
+        ga_ = relu("v" if t < 2 else "s", T.xt2, t, 0, CAPP, 0, [b1[t]], ga)
+    c2 = quant("own", C2, P, T.xt2[:], [ga_, lb], True)
     send(ra, _b(T.h2q[:]), _b(T.ownq[:, C2:C2 + CAPP]), "ha2", hi, [c2])
     send(rb, T.h2s[:], T.owns[:, C2:C2 + CAPP], "hb2", lo, [])
     l2c = quant("lw", P, P, T.xt2[:], [], True)
-    gb = fresh()
-    b0 = CAPP - 1 if last else CAPP
-    for t in (0, 2, 1, 3):
-        gb_ = relu("v" if t < 2 else "s", T.t3, t, b0, P, b0, [ga_], gb)
 
-    n2 = ("n2", 2 * far2)
-    mm(5, "uab", 0, "own", C2, P, True, False, [c2])
-    s2p = mm(5, "uab", P, "srv", N2, P, False, True, [n2])
-    a12 = mm(7, "uab", 0, "lw", 0, 2 * P, True, True, [l1, l2c])
-    b2 = []
-    for t in range(4):
-        mm(t, "wt", P * t, "own", C2, P, True, False, [gb_])
-        b2.append(mm(t, "wt", 512 + P * t, "srv", N2, P, False, True))
+    b2 = [mm(4 + t, "wt", P * t, "own", C2, P, False, True, [c2]) for t in range(4)]
     g2 = fresh()
     for t in range(4):
-        g2_ = relu("s", T.t2, t, 0, P, 0, [b2[t]], g2)
+        g2_ = relu("s" if t % 2 else "v", T.t2, t, 0, P, 0, [b2[t]], g2, 4)
     for t in range(4):
-        mm(t, "wt", P * t, "own", lcol, P, True, False, [g2_, c1r])
+        mm(t, "wt", P * t, "own", lcol, P, True, False, [ga_, c1r])
+    k2 = quant("own", K2, P, T.t2[:], [g2_], True)
+    a12 = mm(7, "uab", 0, "lw", 0, 2 * P, True, True, ua + [g2_, l1, l2c])
+    mm(5, "uab", 0, "own", C2, P, True, False)
+    s2p = mm(5, "uab", P, "srv", N2, P, False, True)
     mm(6, "uab", 0, "own", lcol, P, True, False)
     for k in range(2):
         tt(T.exa[:, P * k:P * k + P], bank(7, P * k, P * k + P), T.maskf[:], A.mult, deps=[a12, CV] if k == 0 else [])
-    s2c = cp(T.s2[:], bank(5), [s2p], True)
     wait("v", [CV])
-    for k in range(2):
-        scan(T.exb[:, P * k:P * k + P], T.hold[:], T.exa[:, P * k:P * k + P], 0.0, A.mult, A.add)
-    fe = tt(T.fl[:], T.s2[:], bank(4), A.is_gt, [s1e, s2c], True)
+    scan(T.exb[:, 0:P], T.hold[:], T.exa[:, 0:P], 0.0, A.mult, A.add)
+    scan(T.exb[:, P:2 * P], T.hold[:], T.exa[:, P:2 * P], 0.0, A.mult, A.add)
+    s2c = cp(T.s2[:], bank(5), [s2p], True)
     m1s = cp(T.m1s[:], T.exb[:, 15:2 * P:16], [CV], True)
     send(rc, T.m1h[:], T.m1s[:], "hc1", lo, [m1s])
-    k2 = quant("own", K2, P, T.t2[:], [g2_], True)
 
-    l2 = ("l2", 2 * far_a)
-    s1l = mm(6, "uab", P, "srv", L2, P, False, True, [l2])
+    l2 = [("l2", 2 * far_a), ("nb", 2 * far_a)]
+    s1l = mm(6, "uab", P, "srv", L2, P, False, True, l2)
     b3 = [mm(t, "wt", 512 + P * t, "srv", L2, P, False, True) for t in range(4)]
-    late = [(0, CAPP - 1, 1), (P - 1, P, 0)] if last else [(0, CAPP, 0)]
+    late = [(0, P - 1, 1), (P - 1, P, 0)] if last else [(0, P, 0)]
     g3 = fresh()
     for t in range(4):
         for a, b, p0 in late:
-            g3_ = relu("s", T.t3, t, a, b, p0, [b3[t], gb_], g3)
+            g3_ = relu("s", T.t3, t, a, b, p0, [b3[t]], g3)
     fa = fresh()
     for a, b, p0 in late:
-        fa_ = tt(T.fl[:, a:b], T.s2[:, a:b], bank(6, p0, p0 + b - a), A.is_gt, [s1l, fe], fa)
-    ts(T.nf[:], T.fl[:], -2.0, A.mult, 2.0, A.add, deps=[fa_])
-    scan(T.cap[:, 0:P], T.fl[:], T.c48[:], 0.0, A.add, A.min)
-    scan(T.cap[:, P:], T.nf[:], T.c96[:], 0.0, A.add, A.min, [CV])
-    tt(T.hh[:, 1:P + 1], T.cap[:, 0:P], T.cap[:, P:], A.add, [CV])
-    tt(T.dd[:], T.hh[:, 1:P + 1], T.hh[:, 0:P], A.subtract, [CV])
-    tt(T.vv[:], T.dd[:], T.maskb[:], A.mult, [CV])
-    k1 = quant("own", K1, P, T.t3[:], [g3_], True)
+        fa_ = tt(T.fl[:, a:b], T.s2[:, a:b], bank(6, p0, p0 + b - a), A.is_gt, [s1l, s2c], fa)
+    scan(T.cap[:, 0:P], T.fl[:], T.c48[:], 0.0, A.add, A.min, [fa_])
+    scan(T.cap[:, P:], T.fl[:], T.gt[:], float(LIFT), A.add, A.max)
+    scan(T.hh[:, 1:P + 1], T.cap[:, 0:P], T.cap[:, P:], float(LIFT), A.min, A.add, [CV])
+    scan(T.dd[:], T.hh[:, 1:P + 1], T.hh[:, 0:P], 0.0, A.max, A.subtract, [CV])
+    scan(T.vv[:], T.dd[:], T.maskb[:], 0.0, A.max, A.mult, [CV])
     scan(T.sc[:], T.d0[:], T.vv[:], -1.0, A.max, A.subtract, [CV])
     o3 = ts(T.off3[:], T.sc[:, 15:P:16], float(P), A.mult, T.col[:, 2:3], A.add, [CV], True)
+    k1 = quant("own", K1, P, T.t3[:], [g3_], True)
     dp = [o3, k1, k2, c2]
     c3 = [pickq("lw", 2 * P, "own", 0, 3 * P, T.off3[:], P, dp), picks("lw", 2 * P, "own", 0, 3 * P, T.off3[:], P, dp)]
     c3s = [pickq("srv", S3, "own", 0, 3 * P, T.off3[:], P, dp), picks("srv", S3, "own", 0, 3 * P, T.off3[:], P, dp)]
     a3 = mm(5, "uab", 0, "lw", 2 * P, P, True, True, c3 + [s2c])
-    bs = mm(6, "uab", P, "srv", 0, SRV, True, True, c3s + [fa_])
-    y23 = mm(4, "u0", 0, "lw", P, 2 * P, True, True, [fe])
+    bs = mm(6, "uab", P, "srv", N2, SRV - N2, True, True, c3s + [fa_])
+    y23 = mm(4, "u0", 0, "lw", P, 2 * P, True, True)
     tt(T.exa[:, 2 * P:], bank(5), T.maskf[:], A.mult, [a3])
     scan(T.exb[:, 2 * P:], T.hold[:], T.exa[:, 2 * P:], 0.0, A.mult, A.add, [CV])
     m3s = cp(T.m3s[:], T.exb[:, 2 * P + 15:3 * P:16], [CV], True)
@@ -326,11 +325,10 @@ def rank_program(g, core, T, topo):
     def src_col(k, p):
         qq = (p + d1) % P
         if k == 0:
-            return S3 + qq
+            return S3 + qq - N2
         if k == 2:
-            return N2 + qq
-        pp = (qq + (1 if last else 0)) % P
-        return L2 + pp if pp < CAPP else N1 + qq
+            return qq
+        return L2 + (qq + (1 if last else 0)) % P - N2
     wait("v", [bs])
     for k in range(3):
         a = 0
@@ -342,8 +340,6 @@ def rank_program(g, core, T, topo):
     wait("v", [CV])
     for k in range(3):
         scan(T.eyb[:, P * k:P * k + P], T.hold[:], T.eya[:, P * k:P * k + P], 0.0, A.mult, A.add)
-    sp3 = cp(T.spb[:, P:2 * P], T.k3t[:].indirect(T.off3[:]), [], True)
-    dma("y", T.sp[0:1, 0:2 * P], T.spb[0:1, 0:2 * P], [sp3])
 
     def sm(k, w=1):
         return T.sm[:, 8 * k:8 * (k + w)]
@@ -364,40 +360,40 @@ def rank_program(g, core, T, topo):
     tt(sm(14), sm(12), sm(10), A.mult)
     tt(sm(0, 2), sm(13, 2), sm(7, 2), A.add, [CV])
     o4 = cp(T.off4[:], sm(0, 2), [CV], True)
-    dp = [o4, n1, n2, l2] + c3s
+    dp = [o4, n1, n2] + l2 + c3s
     oq = pickq("out", 0, "srv", 0, SRV, T.off4[:, 0:8], P, dp)
     osc = picks("out", 0, "srv", 0, SRV, T.off4[:, 0:8], P, dp)
     send(rc, T.lsh[:], T.off4[:, 8:16], "hc4", lo, [o4])
     send(ra, _b(T.h4q[:]), _b(T.outq[:]), "ha4", hi, [oq])
     send(rb, T.h4s[:], T.outs[:], "hb4", lo, [osc])
+    sp3 = cp(T.spb[:, P:2 * P], T.k3t[:].indirect(T.off3[:]), [], True)
 
     ls = ("ls", far_a)
     dp = [ls, l1, l2c] + c3
     lf = [pickq("left", 0, "lw", 0, 3 * P, T.ls[:], P, dp), picks("left", 0, "lw", 0, 3 * P, T.ls[:], P, dp)]
     for t in range(4):
-        mm(t, "wt", 512 + P * t, "right", 0, P, True, False, [g3_, ("r4", 2 * far_a)])
-    b5 = [mm(t, "wt", P * t, "left", 0, P, False, True, lf) for t in range(4)]
+        mm(t, "wt", P * t, "left", 0, P, True, False, [g3_] + lf)
+    b5 = [mm(t, "wt", 512 + P * t, "right", 0, P, False, True, [("r4", 2 * far_a)]) for t in range(4)]
     g5 = fresh()
     for t in range(4):
         g5_ = relu("s", T.t5, t, 0, P, 0, [b5[t]], g5)
-    cp(T.kk[:], T.kt[:].indirect(T.ls[:]))
+    cp(T.kz[:, P:], T.kt[:].indirect(T.ls[:]))
     wait("v", [CV])
     for k in range(3):
-        ts(T.ee[:, P * k:P * k + P], T.kk[:], float(k + 1), A.is_equal)
+        ts(T.ee[:, P * k:P * k + P], T.kz[:, P:], float(k + 1), A.is_equal)
     wait("v", [CV])
     for k in range(3):
         scan(T.cum[:, P * k:P * k + P], T.ee[:, P * k:P * k + P], T.c96[:], 0.0, A.add, A.min)
     tt(T.zz[:], T.cum[:].indirect(T.ls[:]), T.thr[:], A.is_gt, [CV])
     scan(T.sc5[:], T.d0[:], T.zz[:], -1.0, A.max, A.subtract, [CV])
     o5 = ts(T.off5[:], T.sc5[:, 15:P:16], float(P), A.mult, T.col[:, 1:2], A.add, [CV], True)
-    cp(T.tk[:], T.tt[:].indirect(T.off5[:]), [o5])
-    sp4 = tt(T.spb[:, 2 * P:], T.tk[:], T.kk[:], A.mult, [CV], True)
-    dma("y", T.sp[0:1, 2 * P:], T.spb[0:1, 2 * P:], [sp4])
     q5 = quant("lw", 3 * P, P, T.t5[:], [g5_], True)
+    sp4 = op("s", lambda: s_.activation(T.spb[:, 2 * P:], T.kz[:].indirect(T.off5[:]), F.Copy), [o5], True)
     dp = [o5, q5]
     c4q = pickq("c4", 0, "lw", 2 * P, 4 * P, T.off5[:], P, dp)
     c4s = picks("c4", 0, "lw", 2 * P, 4 * P, T.off5[:], P, dp)
     y4 = mm(7, "u0", 0, "c4", 0, P, True, True, [c4q, c4s, m1s])
+    dma("y", T.sp[0:1, :], T.spb[0:1, :], [sp4, sp3])
     dma("y", T.oc[:], _b(T.c4q[:]), [c4q])
     for k in range(4):
         dma("s", T.osc[4 * k:4 * k + 4, :], T.c4s[32 * k:32 * k + 4, :], [c4s])

import numpy as np
from concourse.mybir import dt, AluOpType, ActivationFunctionType

A, F = AluOpType, ActivationFunctionType
P, CAPP = 128, 48
X4, U8, BF, F32, I32, U16 = "float8_e4m3fn_x4", "uint8", "bfloat16", "float32", "int32", "uint16"
K2, C2, K1, C1, C1R, OWN = 0, 128, 256, 384, 528, 656
N1, N2, L2, S3, SRV = 0, 48, 176, 304, 432
REST = P - CAPP
LIFT = 64


def _pair(name, n):
    return {name + "q": ("sbuf", [128, n], X4), name + "s": ("sbuf", [128, n], U8)}


SCRATCH = {"ps": ("psum", [128, 4096], F32)}
for _n, _w in (("wt", 1024), ("u0", 128), ("uab", 256), ("own", OWN), ("srv", SRV), ("lw", 512), ("out", 128),
               ("right", 128), ("left", 128), ("c4", 128), ("h0", REST), ("h1", CAPP), ("h2", CAPP), ("h4", 128)):
    SCRATCH.update(_pair(_n, _w))
for _n, _w, _d in (("xt", 528, BF), ("xt2", 512, BF), ("ut", 512, BF), ("t2", 512, BF), ("t3", 512, BF), ("t5", 512, BF),
                   ("i1", 128, I32), ("i1b", 128, I32), ("i2", 8, I32), ("i3", 1, I32), ("i3b", 1, I32), ("i4", 128, I32),
                   ("maskf", 128, F32), ("maskb", 128, BF), ("thr", 128, BF), ("hold", 128, F32), ("d0", 128, BF),
                   ("col", 4, F32), ("tab", 64, F32), ("kt", 384, BF), ("k3t", 384, BF), ("kz", 256, BF),
                   ("c48", 128, BF), ("c96", 128, BF), ("gt", 128, BF),
                   ("offu", 16, U16), ("off3", 8, U16), ("off4", 16, U16), ("off5", 8, U16),
                   ("s2", 128, F32), ("fl", 128, BF), ("cap", 256, BF), ("hh", 144, BF), ("dd", 128, BF),
                   ("vv", 128, BF), ("sc", 128, BF), ("exa", 384, F32), ("exb", 384, F32), ("eya", 384, F32), ("eyb", 384, F32),
                   ("m1s", 16, F32), ("m3s", 8, F32), ("m1h", 16, F32), ("m3h", 8, F32), ("m1", 16, F32), ("m3", 8, F32),
                   ("lsh", 8, U16), ("ls", 8, U16), ("sm", 128, F32), ("ee", 384, BF), ("cum", 384, BF),
                   ("zz", 128, BF), ("sc5", 128, BF), ("spb", 384, F32), ("yb", 384, F32)):
    SCRATCH[_n] = ("sbuf", [128, _w], _d)

HOPS = ["a1", "a2", "a3", "a4", "b1", "b2", "b4", "c0", "c1", "c4"]
SEMAPHORES = (["cv", "cs", "loc", "n1", "n2", "nb", "l2", "m1", "m3", "r4", "ls"] + ["h" + h for h in HOPS]
              + ["e%d" % i for i in range(110)])


def _mask(engines):
    m = 0
    for e in engines:
        m |= 1 << e
    return m


def _helpers(T, topo, r):
    n = len(T.cores)
    me, prev, nxt = T.cores[r], T.cores[(r - 1) % n], T.cores[(r + 1) % n]
    ok = [c for c in topo.cores_of(me) if c != me and topo.may_write(c, prev) and topo.may_write(c, nxt)]
    ok.sort(key=lambda c: topo.die(c) != topo.die(me))
    return ok[:3]


def _send(g, T, topo, src, dst, out, in_, sem, engines):
    rid, pid = topo.addr(dst, src)
    g.remote_dma(out, in_, T.sem[sem], T.sem.loc, pid, rid, _mask(engines))
    return len(engines)


def _b(v):
    return v.bitcast(dt.uint8)


def _relay(g, core, T, topo, r, role):
    n = len(T.cores)
    prev, nxt = T.cores[(r - 1) % n], T.cores[(r + 1) % n]
    on = len(topo.engines(T.cores[r], core))
    jobs = {0: [("ha1", on // 2, prev, _b(T.srvq[:, N1:N1 + CAPP]), _b(T.h1q[:]), "n1"),
                ("ha2", on // 2, prev, _b(T.srvq[:, L2:L2 + CAPP]), _b(T.h2q[:]), "l2"),
                ("ha3", on, nxt, T.m3[:], T.m3h[:], "m3"),
                ("ha4", on // 2, prev, _b(T.rightq[:]), _b(T.h4q[:]), "r4")],
            1: [("hb1", on // 2, prev, T.srvs[:, N1:N1 + CAPP], T.h1s[:], "n1"),
                ("hb2", on // 2, prev, T.srvs[:, L2:L2 + CAPP], T.h2s[:], "l2"),
                ("hb4", on // 2, prev, T.rights[:], T.h4s[:], "r4")],
            2: [("hc0", on, prev, _b(T.srvq[:, L2 + CAPP:L2 + P]), _b(T.h0q[:]), "nb"),
                ("hc0", 0, prev, T.srvs[:, L2 + CAPP:L2 + P], T.h0s[:], "nb"),
                ("hc1", on // 2, nxt, T.m1[:], T.m1h[:], "m1"),
                ("hc4", on // 2, prev, T.ls[:], T.lsh[:], "ls")]}[role]
    sent = 0
    for sem, cnt, dst, out, in_, rsem in jobs:
        if cnt:
            g.wait_ge(T.sem[sem], cnt)
        sent += _send(g, T, topo, core, dst, out, in_, rsem, topo.engines(core, dst))
    g.wait_ge(T.sem.loc, sent)


def rank_program(g, core, T, topo):
    n = len(T.cores)
    r = T.rank_of(core)
    if r is None:
        for k in range(n):
            h = _helpers(T, topo, k)
            if core in h:
                _relay(g, core, T, topo, k, h.index(core))
        return
    prev2 = T.cores[(r - 2) % n]
    ra, rb, rc = _helpers(T, topo, r)
    on = topo.engines(core, ra)
    lo, hi = on[:len(on) // 2], on[len(on) // 2:]
    far_a = len(topo.engines(_helpers(T, topo, (r + 1) % n)[0], core))
    far2 = len(topo.engines(T.cores[(r + 2) % n], core))
    last = r == n - 1
    d1 = 1 if r == 0 else 0
    d2 = 1 if r < 2 else 0
    scale = float(np.float32(0.05))

    q = {"v": g.vector, "s": g.scalar, "t": g.tensor, "y": g.sync, "g": g}
    cnt, waited, pool = {}, {}, [0]

    def wait(e, toks):
        for s, c in toks:
            if s in ("cv", "cs"):
                c = cnt[s]
            if waited.get((e, s), 0) < c:
                q[e].wait_ge(T.sem[s], c)
                waited[(e, s)] = c

    def fresh():
        pool[0] += 1
        return "e%d" % (pool[0] - 1)

    def op(e, fn, deps=(), sig=None, inc=1):
        wait(e, deps)
        s = "c" + e if sig is None else (fresh() if sig is True else sig)
        fn().then_inc(T.sem[s], inc)
        cnt[s] = cnt.get(s, 0) + inc
        return (s, cnt[s])

    v, s_, pe = g.vector, g.scalar, g.tensor

    def dma(e, out, in_, deps=(), sig=True):
        return op(e, lambda: q[e].dma_start(out, in_), deps, sig, 16)

    def quant(name, c, nn, in_, deps, sig=None):
        return op("v", lambda: v.quantize_mx(T[name + "q"][:, c:c + nn], T[name + "s"][:, c:c + nn], in_), deps, sig)

    def pickq(dst, c, src, a, b, off, nn, deps, sig=True):
        return op("v", lambda: v.tensor_copy(T[dst + "q"][:, c:c + nn].bitcast(dt.uint32),
                                             T[src + "q"][:, a:b].bitcast(dt.uint32).indirect(off)), deps, sig)

    def picks(dst, c, src, a, b, off, nn, deps, sig=True):
        return op("s", lambda: s_.activation(T[dst + "s"][:, c:c + nn], T[src + "s"][:, a:b].indirect(off), F.Copy), deps, sig)

    def bank(b, a=0, e=P):
        return T.ps[:, 512 * b + a:512 * b + e]

    def mm(b, st, sc, mv, mc, nn, start, stop, deps=()):
        def fn():
            return pe.matmul_mx(bank(b, 0, nn), T[st + "q"][:, sc:sc + P], T[st + "s"][:, sc:sc + P],
                                T[mv + "q"][:, mc:mc + nn], T[mv + "s"][:, mc:mc + nn], start, stop)
        if stop:
            return op("t", fn, deps, True)
        wait("t", deps)
        fn()
        return None

    def ts(out, in0, s1, o0, s2=None, o1=None, deps=(), sig=None):
        if o1 is None:
            return op("v", lambda: v.tensor_scalar(out, in0, s1, None, o0), deps, sig)
        return op("v", lambda: v.tensor_scalar(out, in0, s1, s2, o0, o1), deps, sig)

    def tt(out, a, b, o, deps=(), sig=None):
        return op("v", lambda: v.tensor_tensor(out, a, b, o), deps, sig)

    def cp(out, in_, deps=(), sig=None):
        return op("v", lambda: v.tensor_copy(out, in_), deps, sig)

    def ms(out, c, deps=(), sig=None):
        return op("v", lambda: v.memset(out, c), deps, sig)

    def scan(out, a, b, init, o0, o1, deps=(), sig=None):
        return op("v", lambda: v.tensor_tensor_scan(out, a, b, init, o0, o1), deps, sig)

    def relu(e, tile, t, c0, c1, p0, deps, sig, b0=0):
        out, in_ = tile[:, 4 * c0 + t:4 * c1:4], bank(b0 + t, p0, p0 + c1 - c0)
        if e == "v":
            return ts(out, in_, 0.0, A.max, scale, A.mult, deps, sig)
        return op("s", lambda: s_.activation(out, in_, F.Relu, scale=scale), deps, sig)

    sent = [0]

    def send(dst, out, in_, sem, engines, deps):
        wait("g", deps)
        sent[0] += _send(g, T, topo, core, dst, out, in_, sem, engines)

    CV = ("cv", 0)
    lx = [dma("y", T.xt[:, 8:520], T.x[:])]
    if d2:
        lx.append(dma("s", T.xt[:, 520:528], T.x[:, 0:8]))
    lr = dma("s", T.xt[:, 4:8], T.x[:, 508:512]) if last else None
    lwa = dma("y", _b(T.wtq[:, 0:512]), T.wc[:, 0:2048])
    lws = dma("s", T.wts[:], T.ws[:])
    lwb = dma("y", _b(T.wtq[:, 512:]), T.wc[:, 2048:])
    lu = dma("s", T.ut[:], T.u[:])
    io = fresh()
    op("g", lambda: g.iota(T.i1[:], [[1, P]], P, -1), (), io)
    op("g", lambda: g.iota(T.i4[:], [[1, P]], LIFT + 1 - CAPP, 0), (), io)
    op("g", lambda: g.iota(T.i2[:], [[16, 8]], 0, 0), (), io)
    io = op("g", lambda: g.iota(T.i3[:], [[1, 1]], 0, 1), (), io)
    ou = fresh()
    ms(T.offu[:, 0:8], 0, sig=ou)
    ou = ms(T.offu[:, 8:16], 1, sig=ou)
    for k in range(3):
        ms(T.kt[:, P * k:P * k + P], float(k + 1))
        ms(T.k3t[:, P * k:P * k + P], float((k + 2) % 3))
    ms(T.kz[:, 0:P], 0.0)
    ms(T.c48[:], float(CAPP))
    ms(T.c96[:], float(2 * CAPP))
    ms(T.hh[:, 0:16], float(LIFT))
    ms(T.hold[:], 1.0)
    ms(T.d0[:], -100.0)
    ms(T.spb[:, 0:CAPP], 1.0)
    ms(T.spb[:, CAPP:P], 0.0)

    n1c = P + 2 * d2
    c1 = quant("own", C1, n1c, T.xt[:, 8:8 + 4 * n1c], lx, True)
    send(ra, _b(T.h1q[:]), _b(T.ownq[:, C1 + d1:C1 + d1 + CAPP]), "ha1", hi, [c1])
    send(rb, T.h1s[:], T.owns[:, C1 + d1:C1 + d1 + CAPP], "hb1", lo, [])
    e2 = topo.engines(core, prev2)
    send(prev2, _b(T.srvq[:, N2:N2 + P]), _b(T.ownq[:, C1 + d2:C1 + d2 + P]), "n2", e2, [])
    send(prev2, T.srvs[:, N2:N2 + P], T.owns[:, C1 + d2:C1 + d2 + P], "n2", e2, [])
    send(rc, _b(T.h0q[:]), _b(T.ownq[:, C1 + CAPP:C1 + P]), "hc0", hi, [])
    send(rc, T.h0s[:], T.owns[:, C1 + CAPP:C1 + P], "hc0", lo, [])
    lb = cp(T.xt2[:, 4 * CAPP:], T.xt[:, 8 + 4 * CAPP:520], [], True)
    l1 = quant("lw", 0, P, T.xt[:, 8:520], [], True)
    c1r = quant("own", C1R, P, T.xt[:, 4:516], [lr], True) if last else c1
    lcol = C1R if last else C1

    ts(T.i1b[:], T.i1[:], 15, A.bitwise_and, deps=[io])
    ts(T.i3b[:], T.i3[:], 15, A.bitwise_and)
    cp(T.gt[:], T.i4[:])
    ts(T.hold[:, 0:P:16], T.i2[:], 0.0, A.mult, deps=[CV])
    ts(T.d0[:, 0:P:16], T.i2[:], 1.0 / P, A.mult)
    ts(T.maskf[:], T.i1b[:], 0.0, A.is_equal)
    ts(T.maskb[:], T.i1b[:], 0.0, A.is_equal)
    for k in range(3):
        ts(T.col[:, k:k + 1], T.i3b[:], float(P * k), A.add)

    def tab(k):
        return T.tab[:, 8 * k:8 * k + 8]
    t8, qv, pl, o1, o21, tmp, tmp2 = (tab(k) for k in range(7))
    ts(T.thr[:], T.maskf[:], CAPP + 0.5 - 1000.0, A.mult, 1000.0, A.add, deps=[CV])
    ts(t8, T.i2[:], T.col[:, 0:1], A.add)

    def turned(out, in_, d):
        ts(tmp, in_, P - d - 0.5, A.is_gt, -float(P), A.mult, deps=[CV])
        ts(tmp2, in_, float(d), A.add)
        tt(out, tmp, tmp2, A.add, deps=[CV])
    turned(qv, t8, d1)
    turned(pl, qv, 1 if last else 0)
    ts(o1, qv, float(S3), A.add, deps=[CV])
    tt(tmp, pl, qv, A.subtract)
    ts(o21, tmp, float(L2 - S3), A.add, deps=[CV])
    qu = quant("u0", 0, P, T.ut[:], [lu], True)
    ua = [pickq("uab", 0, "u0", 0, P, T.offu[:], 256, [qu, ou]), picks("uab", 0, "u0", 0, P, T.offu[:], 256, [qu, ou])]

    for t in range(4):
        mm(t, "wt", P * t, "own", C1, P, True, False, [lwa, lws, c1])
    n1 = ("n1", 2 * far_a)
    n2 = ("n2", 2 * far2)
    b1 = [mm(t, "wt", 512 + P * t, "srv", N1, P, False, True, [lwb, n1, n2]) for t in (0, 2, 1, 3)]
    b1 = [b1[0], b1[2], b1[1], b1[3]]
    for t in range(4):
        mm(4 + t, "wt", 512 + P * t, "srv", N2, P, True, False)
    ga = fresh()
    for t in (0, 2, 1, 3):
        ga_ = relu("v" if t < 2 else "s", T.xt2, t, 0, CAPP, 0, [b1[t]], ga)
    c2 = quant("own", C2, P, T.xt2[:], [ga_, lb], True)
    send(ra, _b(T.h2q[:]), _b(T.ownq[:, C2:C2 + CAPP]), "ha2", hi, [c2])
    send(rb, T.h2s[:], T.owns[:, C2:C2 + CAPP], "hb2", lo, [])
    l2c = quant("lw", P, P, T.xt2[:], [], True)

    b2 = [mm(4 + t, "wt", P * t, "own", C2, P, False, True, [c2]) for t in range(4)]
    g2 = fresh()
    for t in range(4):
        g2_ = relu("s" if t % 2 else "v", T.t2, t, 0, P, 0, [b2[t]], g2, 4)
    for t in range(4):
        mm(t, "wt", P * t, "own", lcol, P, True, False, [ga_, c1r])
    k2 = quant("own", K2, P, T.t2[:], [g2_], True)
    a12 = mm(7, "uab", 0, "lw", 0, 2 * P, True, True, ua + [g2_, l1, l2c])
    mm(5, "uab", 0, "own", C2, P, True, False)
    s2p = mm(5, "uab", P, "srv", N2, P, False, True)
    mm(6, "uab", 0, "own", lcol, P, True, False)
    for k in range(2):
        tt(T.exa[:, P * k:P * k + P], bank(7, P * k, P * k + P), T.maskf[:], A.mult, deps=[a12, CV] if k == 0 else [])
    wait("v", [CV])
    scan(T.exb[:, 0:P], T.hold[:], T.exa[:, 0:P], 0.0, A.mult, A.add)
    scan(T.exb[:, P:2 * P], T.hold[:], T.exa[:, P:2 * P], 0.0, A.mult, A.add)
    s2c = cp(T.s2[:], bank(5), [s2p], True)
    m1s = cp(T.m1s[:], T.exb[:, 15:2 * P:16], [CV], True)
    send(rc, T.m1h[:], T.m1s[:], "hc1", lo, [m1s])

    l2 = [("l2", 2 * far_a), ("nb", 2 * far_a)]
    s1l = mm(6, "uab", P, "srv", L2, P, False, True, l2)
    b3 = [mm(t, "wt", 512 + P * t, "srv", L2, P, False, True) for t in range(4)]
    late = [(0, P - 1, 1), (P - 1, P, 0)] if last else [(0, P, 0)]
    g3 = fresh()
    for t in range(4):
        for a, b, p0 in late:
            g3_ = relu("s", T.t3, t, a, b, p0, [b3[t]], g3)
    fa = fresh()
    for a, b, p0 in late:
        fa_ = tt(T.fl[:, a:b], T.s2[:, a:b], bank(6, p0, p0 + b - a), A.is_gt, [s1l, s2c], fa)
    scan(T.cap[:, 0:P], T.fl[:], T.c48[:], 0.0, A.add, A.min, [fa_])
    scan(T.cap[:, P:], T.fl[:], T.gt[:], float(LIFT), A.add, A.max)
    scan(T.hh[:, 1:P + 1], T.cap[:, 0:P], T.cap[:, P:], float(LIFT), A.min, A.add, [CV])
    scan(T.dd[:], T.hh[:, 1:P + 1], T.hh[:, 0:P], 0.0, A.max, A.subtract, [CV])
    scan(T.vv[:], T.dd[:], T.maskb[:], 0.0, A.max, A.mult, [CV])
    scan(T.sc[:], T.d0[:], T.vv[:], -1.0, A.max, A.subtract, [CV])
    o3 = ts(T.off3[:], T.sc[:, 15:P:16], float(P), A.mult, T.col[:, 2:3], A.add, [CV], True)
    k1 = quant("own", K1, P, T.t3[:], [g3_], True)
    dp = [o3, k1, k2, c2]
    c3 = [pickq("lw", 2 * P, "own", 0, 3 * P, T.off3[:], P, dp), picks("lw", 2 * P, "own", 0, 3 * P, T.off3[:], P, dp)]
    c3s = [pickq("srv", S3, "own", 0, 3 * P, T.off3[:], P, dp), picks("srv", S3, "own", 0, 3 * P, T.off3[:], P, dp)]
    a3 = mm(5, "uab", 0, "lw", 2 * P, P, True, True, c3 + [s2c])
    bs = mm(6, "uab", P, "srv", N2, SRV - N2, True, True, c3s + [fa_])
    y23 = mm(4, "u0", 0, "lw", P, 2 * P, True, True)
    tt(T.exa[:, 2 * P:], bank(5), T.maskf[:], A.mult, [a3])
    scan(T.exb[:, 2 * P:], T.hold[:], T.exa[:, 2 * P:], 0.0, A.mult, A.add, [CV])
    m3s = cp(T.m3s[:], T.exb[:, 2 * P + 15:3 * P:16], [CV], True)
    send(ra, T.m3h[:], T.m3s[:], "ha3", on, [m3s])
    yc = op("s", lambda: s_.activation(T.yb[:, 0:2 * P], bank(4, 0, 2 * P), F.Copy), [y23], True)
    dma("y", T.y[:, 0:2 * P], T.yb[:, 0:2 * P], [yc])

    def src_col(k, p):
        qq = (p + d1) % P
        if k == 0:
            return S3 + qq - N2
        if k == 2:
            return qq
        return L2 + (qq + (1 if last else 0)) % P - N2
    wait("v", [bs])
    for k in range(3):
        a = 0
        for p in range(1, P + 1):
            if p == P or src_col(k, p) != src_col(k, p - 1) + 1:
                c = src_col(k, a)
                tt(T.eya[:, P * k + a:P * k + p], bank(6, c, c + p - a), T.maskf[:, a:p], A.mult)
                a = p
    wait("v", [CV])
    for k in range(3):
        scan(T.eyb[:, P * k:P * k + P], T.hold[:], T.eya[:, P * k:P * k + P], 0.0, A.mult, A.add)

    def sm(k, w=1):
        return T.sm[:, 8 * k:8 * (k + w)]
    tt(sm(0, 2), T.m1[:], T.eyb[:, 15:2 * P:16], A.add, [("m1", far_a), CV])
    cp(sm(2), T.eyb[:, 2 * P + 15:3 * P:16])
    tt(sm(3), sm(1), sm(0), A.is_gt, [CV])
    tt(sm(4), sm(1), sm(0), A.max)
    tt(sm(5), sm(3), o21, A.mult, [CV])
    ts(sm(6), sm(3), float(P), A.mult)
    tt(sm(7), sm(5), o1, A.add, [CV])
    tt(sm(8), sm(6), t8, A.add)
    ts(sm(9), sm(5), -1.0, A.mult, float(N2 - S3), A.add)
    ts(sm(10), sm(6), -1.0, A.mult, float(2 * P), A.add)
    wait("v", [CV])
    tt(sm(11), T.m3[:], sm(2), A.add, [("m3", far_a)])
    tt(sm(12), sm(11), sm(4), A.is_gt, [CV])
    tt(sm(13), sm(12), sm(9), A.mult, [CV])
    tt(sm(14), sm(12), sm(10), A.mult)
    tt(sm(0, 2), sm(13, 2), sm(7, 2), A.add, [CV])
    o4 = cp(T.off4[:], sm(0, 2), [CV], True)
    dp = [o4, n1, n2] + l2 + c3s
    oq = pickq("out", 0, "srv", 0, SRV, T.off4[:, 0:8], P, dp)
    osc = picks("out", 0, "srv", 0, SRV, T.off4[:, 0:8], P, dp)
    send(rc, T.lsh[:], T.off4[:, 8:16], "hc4", lo, [o4])
    send(ra, _b(T.h4q[:]), _b(T.outq[:]), "ha4", hi, [oq])
    send(rb, T.h4s[:], T.outs[:], "hb4", lo, [osc])
    sp3 = cp(T.spb[:, P:2 * P], T.k3t[:].indirect(T.off3[:]), [], True)

    ls = ("ls", far_a)
    dp = [ls, l1, l2c] + c3
    lf = [pickq("left", 0, "lw", 0, 3 * P, T.ls[:], P, dp), picks("left", 0, "lw", 0, 3 * P, T.ls[:], P, dp)]
    for t in range(4):
        mm(t, "wt", P * t, "left", 0, P, True, False, [g3_] + lf)
    b5 = [mm(t, "wt", 512 + P * t, "right", 0, P, False, True, [("r4", 2 * far_a)]) for t in range(4)]
    g5 = fresh()
    for t in range(4):
        g5_ = relu("s", T.t5, t, 0, P, 0, [b5[t]], g5)
    cp(T.kz[:, P:], T.kt[:].indirect(T.ls[:]))
    wait("v", [CV])
    for k in range(3):
        ts(T.ee[:, P * k:P * k + P], T.kz[:, P:], float(k + 1), A.is_equal)
    wait("v", [CV])
    for k in range(3):
        scan(T.cum[:, P * k:P * k + P], T.ee[:, P * k:P * k + P], T.c96[:], 0.0, A.add, A.min)
    tt(T.zz[:], T.cum[:].indirect(T.ls[:]), T.thr[:], A.is_gt, [CV])
    scan(T.sc5[:], T.d0[:], T.zz[:], -1.0, A.max, A.subtract, [CV])
    o5 = ts(T.off5[:], T.sc5[:, 15:P:16], float(P), A.mult, T.col[:, 1:2], A.add, [CV], True)
    q5 = quant("lw", 3 * P, P, T.t5[:], [g5_], True)
    sp4 = op("s", lambda: s_.activation(T.spb[:, 2 * P:], T.kz[:].indirect(T.off5[:]), F.Copy), [o5], True)
    dp = [o5, q5]
    c4q = pickq("c4", 0, "lw", 2 * P, 4 * P, T.off5[:], P, dp)
    c4s = picks("c4", 0, "lw", 2 * P, 4 * P, T.off5[:], P, dp)
    y4 = mm(7, "u0", 0, "c4", 0, P, True, True, [c4q, c4s, m1s])
    dma("y", T.sp[0:1, :], T.spb[0:1, :], [sp4, sp3])
    dma("y", T.oc[:], _b(T.c4q[:]), [c4q])
    for k in range(4):
        dma("s", T.osc[4 * k:4 * k + 4, :], T.c4s[32 * k:32 * k + 4, :], [c4s])
    y4c = cp(T.yb[:, 2 * P:], bank(7), [y4], True)
    dma("y", T.y[:, 2 * P:], T.yb[:, 2 * P:], [y4c])

    g.wait_ge(T.sem.loc, sent[0])
    for s, c in cnt.items():
        if max([w for (e, s2), w in waited.items() if s2 == s] + [0]) < c:
            wait(s[1] if s in ("cv", "cs") else "g", [(s, c)])
